import numpy as np
import ml_dtypes


def mxq(x, axis, fmt="e4m3"):
    dtype, down = {"e4m3": (ml_dtypes.float8_e4m3fn, 7), "e5m2": (ml_dtypes.float8_e5m2, 14)}[fmt]
    v = np.moveaxis(np.asarray(x, np.float32).astype(ml_dtypes.bfloat16).astype(np.float64), axis, -1)
    blocks = v.reshape(v.shape[:-1] + (-1, 32))
    amax = np.abs(blocks).max(-1, keepdims=True)
    byte = np.maximum(np.where(amax > 0, np.frexp(amax)[1] - 1 + 127, 0) - down, 1)
    scale = np.exp2(byte - 127.0)
    codes = (blocks / scale).astype(np.float32).astype(dtype).astype(np.float64)
    return np.moveaxis((codes * scale).reshape(v.shape), -1, axis)


WIDE = False


def mx_kscale(k):
    if not WIDE:
        return np.ones(k)
    levels = np.array([30, -30])
    if k % 512:
        return np.exp2(np.random.permutation(np.resize(levels, k // 32))).repeat(32)
    a = np.empty((k // 512, 16))
    for p in range(k // 512):
        a[p, :8] = np.random.permutation(np.resize(levels, 8))
        for g in range(8):
            far = levels[np.abs(levels - a[p, g]) >= 10]
            a[p, g + 8] = far[np.random.randint(len(far))]
    return np.exp2(a.ravel()).repeat(32)


def f64(x):
    return np.asarray(x).astype(np.float64)


def striped(idx):
    return np.tile(idx.reshape(-1, 16).T, (8, 1)).astype(np.uint16)


def unstriped(offs):
    return offs[:16].T.reshape(-1).astype(np.int64)


E2M1 = np.array([0.0, 0.5, 1.0, 1.5, 2.0, 3.0, 4.0, 6.0, -0.0, -0.5, -1.0, -1.5, -2.0, -3.0, -4.0, -6.0])


def pack_weight(w, fmt):
    k, n = w.shape
    w = f64(np.asarray(w, np.float32).astype(ml_dtypes.bfloat16)).reshape(k // 32, 32, n)
    amax = np.abs(w).max(1)
    if fmt == "e4m3":
        byte = np.frexp(amax)[1] - 1 + 127 - 7
    elif fmt == "e5m2":
        byte = np.frexp(amax)[1] - 1 + 127 - 14
    else:
        mant, ex = np.frexp(amax / 6.0)
        byte = np.where(mant > 0.5, ex, ex - 1) + 127
    byte = np.clip(np.where(amax > 0, byte, 1), 1, 254)
    scaled = (w * np.exp2(127.0 - byte)[:, None, :]).reshape(k, n).astype(np.float32)
    by_word = np.ascontiguousarray(scaled.reshape(k // 512, 128, 4, n).transpose(0, 1, 3, 2))
    if fmt == "e4m3":
        words = by_word.astype(ml_dtypes.float8_e4m3fn).view(np.uint8)
    elif fmt == "e5m2":
        words = by_word.astype(ml_dtypes.float8_e5m2).view(np.uint8)
    else:
        c = by_word.astype(ml_dtypes.float4_e2m1fn).view(np.uint8) & 0xF
        words = (c[..., 0::2] | (c[..., 1::2] << 4)).reshape(k // 512, 128, 2 * n)
    return np.ascontiguousarray(words), np.ascontiguousarray(byte.astype(np.uint8).reshape(k // 512, 16, n))


def unpack_weight(words, scales, fmt):
    g, _, n = scales.shape
    words = np.ascontiguousarray(words).reshape(g, 128, n, -1)
    if fmt == "e4m3":
        vals = words.view(ml_dtypes.float8_e4m3fn).astype(np.float64)
    elif fmt == "e5m2":
        vals = words.view(ml_dtypes.float8_e5m2).astype(np.float64)
    else:
        nib = np.empty((g, 128, n, 4), np.uint8)
        nib[..., 0::2] = words & 0xF
        nib[..., 1::2] = words >> 4
        vals = E2M1[nib]
    vals = vals * np.repeat(np.exp2(scales.astype(np.float64) - 127.0), 8, axis=1)[..., None]
    return vals.transpose(0, 1, 3, 2).reshape(g * 512, n)


def d_relu(v):
    return (v > 0).astype(np.float64)


K, T, E, C, H, N = 512, 1024, 4, 512, 512, 512


def by_expert(wq, xq):
    return np.concatenate([wq[e].T @ xq[:, e * C:(e + 1) * C] for e in range(E)], axis=1)


def setup_inputs():
    n = np.random.standard_normal
    v = mx_kscale(N)
    u = mx_kscale(H)
    first = np.random.permutation(np.repeat(np.arange(E), T // E))
    second = (first + 1 + np.random.permutation(np.repeat(np.arange(E - 1), -(-T // (E - 1)))[:T])) % E
    while np.bincount(second, minlength=E).max() != T // E:
        load = np.bincount(second, minlength=E); hi, lo = int(load.argmax()), int(load.argmin())
        t = np.flatnonzero((second == hi) & (first != lo))[0]; second[t] = lo
    slot_token = np.empty(E * C, np.int64); pos = np.empty((2, T), np.int64); fill = np.zeros(E, np.int64)
    place = np.stack([np.random.permutation(C) for _ in range(E)])
    for r, deal in enumerate((first, second)):
        for t in np.random.permutation(T):
            e = deal[t]; j = e * C + place[e, fill[e]]; fill[e] += 1; slot_token[j] = t; pos[r, t] = j
    g = np.random.uniform(0.2, 0.8, T)
    w_slot = np.empty(E * C); w_slot[pos[0]] = g; w_slot[pos[1]] = 1.0 - g
    dy = pack_weight(n((N, T)) * v[:, None], "e5m2")
    w2t = pack_weight(n((N, H)) / np.sqrt(N) / v[:, None] * u, "e2m1")
    w1t = [pack_weight(m, "e2m1") for m in n((E, H, K)) / np.sqrt(H) / u[None, :, None]]
    return {
        "dy_words": dy[0],
        "dy_scales": dy[1],
        "w2t_words": w2t[0],
        "w2t_scales": w2t[1],
        "w1t_words": np.stack([m[0] for m in w1t]),
        "w1t_scales": np.stack([m[1] for m in w1t]),
        "a": (n((H, E * C))).astype(np.float32),
        "gate": (np.tile(w_slot, (128, 1))).astype(np.float32),
        "offs": striped(slot_token),
        "pos1": striped(pos[0]),
        "pos2": striped(pos[1]),
    }


def reference(dy_words, dy_scales, w2t_words, w2t_scales, w1t_words, w1t_scales, a, gate, offs, pos1, pos2):
    w2t = unpack_weight(w2t_words, w2t_scales, "e2m1")
    w1t = np.stack([unpack_weight(w1t_words[e], w1t_scales[e], "e2m1") for e in range(E)])
    idx = unstriped(offs)
    dc = w2t.T @ unpack_weight(dy_words, dy_scales, "e5m2")
    da = f64(gate[:1]) * dc[:, idx] * d_relu(f64(a))
    dx = by_expert(w1t, mxq(da, 0, "e5m2"))
    out = dx[:, unstriped(pos1)] + dx[:, unstriped(pos2)]
    return out

@@ -1,0 +1,188 @@
+from contextlib import ExitStack
+
+import concourse.mybir as mybir
+
+K, T, E, C, H, N = 512, 1024, 4, 512, 512, 512
+S = E * C
+P = 128
+PACK = 4
+FLOPS = 2 * N * H * T + 2 * H * K * S
+
+F32 = mybir.dt.float32
+BF16 = mybir.dt.bfloat16
+I32 = mybir.dt.int32
+U32 = mybir.dt.uint32
+U16 = mybir.dt.uint16
+U8 = mybir.dt.uint8
+FP4X4 = mybir.dt.float4_e2m1fn_x4
+E5X4 = mybir.dt.float8_e5m2_x4
+ALU = mybir.AluOpType
+
+
+def tile_moe_sdb_relu_kernel(
+    tc, dy_words, dy_scales, w2t_words, w2t_scales, w1t_words, w1t_scales, a, gate, offs, pos1, pos2, out
+):
+    nc = tc.nc
+    with ExitStack() as ctx:
+        keep = ctx.enter_context(tc.tile_pool(name="keep", bufs=1))
+        ring = ctx.enter_context(tc.tile_pool(name="ring", bufs=2))
+        psum = ctx.enter_context(tc.psum_pool(name="psum", bufs=8))
+
+        offs_t = keep.tile([P, S // 16], U16, name="offs_t")
+        pos1_t = keep.tile([P, T // 16], U16, name="pos1_t")
+        pos2_t = keep.tile([P, T // 16], U16, name="pos2_t")
+        w2_raw = keep.tile([P, 2 * H], U8, name="w2_raw", align_bytes=64)
+        w2_codes = keep.tile([P, 2 * H], U8, name="w2_codes", align_bytes=64)
+        w2s_raw = keep.tile([P, H], U8, name="w2s_raw", align_bytes=64)
+        w2_scale = keep.tile([P, H], U8, name="w2_scale", align_bytes=64)
+        dy_codes = keep.tile([P, T], U32, name="dy_codes", align_bytes=64)
+        dy_scale = keep.tile([P, T], U8, name="dy_scale", align_bytes=64)
+        w1_codes = keep.tile([P, E, 2 * K], U8, name="w1_codes", align_bytes=64)
+        w1_scale = keep.tile([P, E, K], U8, name="w1_scale", align_bytes=64)
+        gate_t = [keep.tile([P, C], F32, name="gate%d" % e) for e in range(E)]
+        a_t = [[keep.tile([P, C], F32, name="a%d_%d" % (e, j)) for j in range(PACK)] for e in range(E)]
+        m_t = [[keep.tile([P, C], F32, name="m%d_%d" % (e, j)) for j in range(PACK)] for e in range(E)]
+        dc = [keep.tile([P, T], F32, name="dc%d" % j) for j in range(PACK)]
+        dx = [keep.tile([P, S], F32, name="dx%d" % kt) for kt in range(K // P)]
+        da_codes = [keep.tile([P, C], U32, name="dac%d" % e, align_bytes=64) for e in range(E)]
+        da_scale = [keep.tile([P, C], U8, name="das%d" % e, align_bytes=64) for e in range(E)]
+
+        nc.vector.memset(w2s_raw[:].bitcast(I32), 0)
+        nc.vector.memset(dy_scale[:].bitcast(I32), 0)
+        nc.vector.memset(w1_scale[:].rearrange("p e k -> p (e k)").bitcast(I32), 0)
+
+        a_rows = a.rearrange("(p j) s -> p j s", j=PACK)
+
+        def load_scale_rows(plane, rows, q):
+            nc.sync.dma_start(plane[32 * q : 32 * q + 4, :].bitcast(I32), rows[4 * q : 4 * q + 4, :].bitcast(I32))
+
+        def load_expert(e):
+            nc.sync.dma_start(gate_t[e][:], gate[:, e * C : (e + 1) * C])
+            for j in range(PACK):
+                nc.sync.dma_start(a_t[e][j][:], a_rows[:, j, e * C : (e + 1) * C])
+
+        for q in range(4):
+            load_scale_rows(w2s_raw, w2t_scales[0], q)
+        nc.sync.dma_start(w2_raw[:].bitcast(I32), w2t_words[0].bitcast(I32))
+        nc.sync.dma_start(dy_codes[:].bitcast(I32), dy_words[0].rearrange("p t d -> p (t d)").bitcast(I32))
+        for q in range(4):
+            load_scale_rows(dy_scale, dy_scales[0], q)
+        nc.sync.dma_start(offs_t[:], offs)
+        load_expert(0)
+        load_expert(1)
+        for q in range(4):
+            nc.sync.dma_start(
+                w1_scale[32 * q : 32 * q + 4, :, :].bitcast(I32),
+                w1t_scales[:, 0, 4 * q : 4 * q + 4, :].rearrange("e r k -> r e k").bitcast(I32),
+            )
+        nc.sync.dma_start(w1_codes[:].bitcast(I32), w1t_words[:, 0].rearrange("e p b -> p e b").bitcast(I32))
+        load_expert(2)
+        load_expert(3)
+        nc.sync.dma_start(pos1_t[:], pos1)
+        nc.sync.dma_start(pos2_t[:], pos2)
+
+        for lo, hi in ((0, 1), (1, PACK)):
+            nc.vector.tensor_copy(
+                w2_codes[:].bitcast(U16).rearrange("p (j m) -> p j m", j=PACK)[:, lo:hi, :],
+                w2_raw[:].bitcast(U16).rearrange("p (m j) -> p j m", j=PACK)[:, lo:hi, :],
+            )
+            nc.vector.tensor_copy(
+                w2_scale[:].rearrange("p (j m) -> p j m", j=PACK)[:, lo:hi, :],
+                w2s_raw[:].rearrange("p (m j) -> p j m", j=PACK)[:, lo:hi, :],
+            )
+
+        for j in range(PACK):
+            for h in range(T // 512):
+                cols = slice(512 * h, 512 * (h + 1))
+                acc = psum.tile([P, 512], F32, name="acc")
+                nc.tensor.matmul_mx(
+                    out=acc[:],
+                    lhsT=w2_codes[:, 2 * P * j : 2 * P * (j + 1)].bitcast(FP4X4),
+                    lhsT_scale=w2_scale[:, P * j : P * (j + 1)],
+                    rhs=dy_codes[:, cols].bitcast(E5X4),
+                    rhs_scale=dy_scale[:, cols],
+                    start=True,
+                    stop=True,
+                )
+                nc.scalar.copy(dc[j][:, cols], acc[:])
+
+        def masked_gate(e, j):
+            nc.vector.scalar_tensor_tensor(m_t[e][j][:], a_t[e][j][:], 0.0, gate_t[e][:], ALU.is_gt, ALU.mult)
+
+        def gather_piece(e, lo, hi):
+            y = ring.tile([P, PACK, hi - lo], F32, name="y", bufs=3)
+            s0 = e * C + lo
+            for j in range(PACK):
+                nc.vector.tensor_tensor(
+                    y[:, j, :], dc[j][:].indirect(offs_t[:, s0 // 16 : (s0 + hi - lo) // 16]), m_t[e][j][:, lo:hi], ALU.mult
+                )
+            return y
+
+        def round_piece(y, on_vector):
+            width = y.shape[2]
+            da = ring.tile([P, width, PACK], BF16, name="da", align_bytes=64, bufs=3)
+            if on_vector:
+                nc.vector.tensor_copy(da[:], y[:].rearrange("p j s -> p s j"))
+            else:
+                nc.scalar.copy(da[:], y[:].rearrange("p j s -> p s j"))
+            return da
+
+        def quantize_piece(da, e, lo, hi):
+            nc.vector.quantize_mx(
+                out=da_codes[e][:, lo:hi].bitcast(E5X4),
+                scales=da_scale[e][:, lo:hi],
+                in_=da[:].rearrange("p s j -> p (s j)"),
+            )
+
+        def expert_product(e, kt):
+            acc = psum.tile([P, C], F32, name="acc")
+            nc.tensor.matmul_mx(
+                out=acc[:],
+                lhsT=w1_codes[:, e, 2 * P * kt : 2 * P * (kt + 1)].bitcast(FP4X4),
+                lhsT_scale=w1_scale[:, e, P * kt : P * (kt + 1)],
+                rhs=da_codes[e][:].bitcast(E5X4),
+                rhs_scale=da_scale[e][:],
+                start=True,
+                stop=True,
+            )
+            nc.scalar.copy(dx[kt][:, e * C : (e + 1) * C], acc[:])
+
+        pieces = [(0, 0, 512), (1, 0, 512), (2, 0, 512), (3, 0, 256), (3, 256, 384), (3, 384, 512)]
+        pending = None
+        for e, lo, hi in pieces:
+            if lo == 0:
+                for j in range(PACK):
+                    masked_gate(e, j)
+            y = gather_piece(e, lo, hi)
+            if pending is not None:
+                quantize_piece(*pending)
+                if pending[3] == C:
+                    expert_product(pending[1], 0)
+            pending = (round_piece(y, (e, hi) == (E - 1, C)), e, lo, hi)
+        quantize_piece(*pending)
+        expert_product(E - 1, 0)
+
+        def fetch(kt, lo, hi):
+            first = ring.tile([P, hi - lo], F32, name="first", bufs=3)
+            second = ring.tile([P, hi - lo], F32, name="second", bufs=3)
+            nc.vector.tensor_copy(first[:], dx[kt][:].indirect(pos1_t[:, lo // 16 : hi // 16]))
+            nc.vector.tensor_copy(second[:], dx[kt][:].indirect(pos2_t[:, lo // 16 : hi // 16]))
+            return first, second
+
+        def combine(first, second, kt, lo, hi, last):
+            total = ring.tile([P, hi - lo], F32, name="total", bufs=3)
+            engine = nc.vector
+            engine.tensor_tensor(total[:], first[:], second[:], ALU.add)
+            nc.sync.dma_start(out[kt * P : (kt + 1) * P, lo:hi], total[:])
+
+        spans = [(0, 0, 1024), (1, 0, 1024), (2, 0, 1024), (3, 0, 512), (3, 512, 768), (3, 768, 1024)]
+        waiting = None
+        for kt, lo, hi in spans:
+            if lo == 0 and kt + 1 < K // P:
+                for e in range(E):
+                    expert_product(e, kt + 1)
+            pair = fetch(kt, lo, hi)
+            if waiting is not None:
+                combine(*waiting, False)
+            waiting = (pair[0], pair[1], kt, lo, hi)
+        combine(*waiting, True)

@@ -171,7 +171,7 @@ def tile_moe_sdb_relu_kernel(
 
         def combine(first, second, kt, lo, hi, last):
             total = ring.tile([P, hi - lo], F32, name="total", bufs=3)
-            engine = nc.vector
+            engine = nc.vector if last else nc.gpsimd
             engine.tensor_tensor(total[:], first[:], second[:], ALU.add)
             nc.sync.dma_start(out[kt * P : (kt + 1) * P, lo:hi], total[:])
 

@@ -1,6 +1,7 @@
 from contextlib import ExitStack
 
 import concourse.mybir as mybir
+from concourse.masks import make_identity
 
 K, T, E, C, H, N = 512, 1024, 4, 512, 512, 512
 S = E * C
@@ -17,6 +18,9 @@ U8 = mybir.dt.uint8
 FP4X4 = mybir.dt.float4_e2m1fn_x4
 E5X4 = mybir.dt.float8_e5m2_x4
 ALU = mybir.AluOpType
+ACT = mybir.ActivationFunctionType
+TAIL = 512
+HEAD_PART = 256
 
 
 def tile_moe_sdb_relu_kernel(
@@ -26,7 +30,8 @@ def tile_moe_sdb_relu_kernel(
     with ExitStack() as ctx:
         keep = ctx.enter_context(tc.tile_pool(name="keep", bufs=1))
         ring = ctx.enter_context(tc.tile_pool(name="ring", bufs=2))
-        psum = ctx.enter_context(tc.psum_pool(name="psum", bufs=8))
+        share = ctx.enter_context(tc.tile_pool(name="share", bufs=1))
+        psum = ctx.enter_context(tc.psum_pool(name="psum", bufs=4))
 
         offs_t = keep.tile([P, S // 16], U16, name="offs_t")
         pos1_t = keep.tile([P, T // 16], U16, name="pos1_t")
@@ -39,36 +44,58 @@ def tile_moe_sdb_relu_kernel(
         dy_scale = keep.tile([P, T], U8, name="dy_scale", align_bytes=64)
         w1_codes = keep.tile([P, E, 2 * K], U8, name="w1_codes", align_bytes=64)
         w1_scale = keep.tile([P, E, K], U8, name="w1_scale", align_bytes=64)
-        gate_t = [keep.tile([P, C], F32, name="gate%d" % e) for e in range(E)]
-        a_t = [[keep.tile([P, C], F32, name="a%d_%d" % (e, j)) for j in range(PACK)] for e in range(E)]
-        m_t = [[keep.tile([P, C], F32, name="m%d_%d" % (e, j)) for j in range(PACK)] for e in range(E)]
+        ident = keep.tile([P, P], F32, name="ident")
+        gate_rows = keep.tile([P, P], F32, name="gate_rows")
+        gate_cols = keep.tile([P, S // P], F32, name="gate_cols")
+        gate_tail = keep.tile([P, TAIL], F32, name="gate_tail")
+        a_tail = keep.tile([P, PACK, HEAD_PART], F32, name="a_tail")
+        m_tail = keep.tile([P, PACK, HEAD_PART], F32, name="m_tail")
+        widths = [C, C, C]
+        a_pool = keep.tile([P, PACK, TAIL - HEAD_PART], F32, name="a_pool")
+        sign_pool = keep.tile([P, PACK, TAIL - HEAD_PART], BF16, name="sign_pool")
+        mask_pool = keep.tile([P, PACK, TAIL - HEAD_PART], BF16, name="mask_pool")
+        m_pool = keep.tile([P, PACK, TAIL - HEAD_PART], F32, name="m_pool")
+        a_t = [
+            [share.tile([P, PACK, C // 2], F32, name="a", tag="picked%d" % (h + 1) if e == 0 else "a%d_%d" % (e, h), align_bytes=64) for h in range(2)]
+            for e in range(E - 1)
+        ]
+        sign_t = [keep.tile([P, PACK, widths[e]], BF16, name="sign%d" % e) for e in range(E - 1)]
+        mask_t = [share.tile([P, widths[e], PACK], BF16, name="mask%d" % e, tag="after_mask%d" % e) for e in range(E - 1)]
         dc = [keep.tile([P, T], F32, name="dc%d" % j) for j in range(PACK)]
         dx = [keep.tile([P, S], F32, name="dx%d" % kt) for kt in range(K // P)]
-        da_codes = [keep.tile([P, C], U32, name="dac%d" % e, align_bytes=64) for e in range(E)]
-        da_scale = [keep.tile([P, C], U8, name="das%d" % e, align_bytes=64) for e in range(E)]
+        lead = [0] * (E - 1) + [P]
+        da_codes = [keep.tile([P, lead[e] + C], U32, name="dac%d" % e, align_bytes=64) for e in range(E)]
+        da_scale = [keep.tile([P, lead[e] + C], U8, name="das%d" % e, align_bytes=64) for e in range(E)]
 
-        nc.vector.memset(w2s_raw[:].bitcast(I32), 0)
-        nc.vector.memset(dy_scale[:].bitcast(I32), 0)
+        nc.gpsimd.memset(w2s_raw[:].bitcast(I32), 0)
+        nc.gpsimd.memset(dy_scale[:].bitcast(I32), 0)
         nc.vector.memset(w1_scale[:].rearrange("p e k -> p (e k)").bitcast(I32), 0)
+        nc.vector.memset(da_codes[E - 1][:, :P].bitcast(I32), 0)
+        nc.vector.memset(da_scale[E - 1][:, :P].bitcast(I32), 0)
 
         a_rows = a.rearrange("(p j) s -> p j s", j=PACK)
 
-        def load_scale_rows(plane, rows, q):
-            nc.sync.dma_start(plane[32 * q : 32 * q + 4, :].bitcast(I32), rows[4 * q : 4 * q + 4, :].bitcast(I32))
+        def load_scale_rows(queue, plane, rows, q):
+            queue.dma_start(plane[32 * q : 32 * q + 4, :].bitcast(I32), rows[4 * q : 4 * q + 4, :].bitcast(I32))
 
         def load_expert(e):
-            nc.sync.dma_start(gate_t[e][:], gate[:, e * C : (e + 1) * C])
-            for j in range(PACK):
-                nc.sync.dma_start(a_t[e][j][:], a_rows[:, j, e * C : (e + 1) * C])
+            for h in range(2):
+                nc.sync.dma_start(a_t[e][h][:], a_rows[:, :, e * C + h * C // 2 : e * C + (h + 1) * C // 2])
 
         for q in range(4):
-            load_scale_rows(w2s_raw, w2t_scales[0], q)
+            load_scale_rows(nc.sync, w2s_raw, w2t_scales[0], q)
         nc.sync.dma_start(w2_raw[:].bitcast(I32), w2t_words[0].bitcast(I32))
         nc.sync.dma_start(dy_codes[:].bitcast(I32), dy_words[0].rearrange("p t d -> p (t d)").bitcast(I32))
         for q in range(4):
-            load_scale_rows(dy_scale, dy_scales[0], q)
+            load_scale_rows(nc.sync, dy_scale, dy_scales[0], q)
+        make_identity(nc, ident[:])
         nc.sync.dma_start(offs_t[:], offs)
+        nc.sync.dma_start(gate_tail[:, TAIL - HEAD_PART :], gate[:, S - HEAD_PART :])
+        nc.sync.dma_start(a_tail[:], a_rows[:, :, S - HEAD_PART :])
+        nc.sync.dma_start(gate_rows[:], gate[0 : P * P // S, :].rearrange("r (c s) -> (r c) s", s=P))
         load_expert(0)
+        nc.sync.dma_start(gate_tail[:, : TAIL - HEAD_PART], gate[:, S - TAIL : S - HEAD_PART])
+        nc.sync.dma_start(a_pool[:], a_rows[:, :, S - TAIL : S - HEAD_PART])
         load_expert(1)
         for q in range(4):
             nc.sync.dma_start(
@@ -77,7 +104,6 @@ def tile_moe_sdb_relu_kernel(
             )
         nc.sync.dma_start(w1_codes[:].bitcast(I32), w1t_words[:, 0].rearrange("e p b -> p e b").bitcast(I32))
         load_expert(2)
-        load_expert(3)
         nc.sync.dma_start(pos1_t[:], pos1)
         nc.sync.dma_start(pos2_t[:], pos2)
 
@@ -94,7 +120,7 @@ def tile_moe_sdb_relu_kernel(
         for j in range(PACK):
             for h in range(T // 512):
                 cols = slice(512 * h, 512 * (h + 1))
-                acc = psum.tile([P, 512], F32, name="acc")
+                acc = psum.tile([P, 512], F32, name="acc", tag=("turned", "back")[h])
                 nc.tensor.matmul_mx(
                     out=acc[:],
                     lhsT=w2_codes[:, 2 * P * j : 2 * P * (j + 1)].bitcast(FP4X4),
@@ -106,61 +132,152 @@ def tile_moe_sdb_relu_kernel(
                 )
                 nc.scalar.copy(dc[j][:, cols], acc[:])
 
-        def masked_gate(e, j):
-            nc.vector.scalar_tensor_tensor(m_t[e][j][:], a_t[e][j][:], 0.0, gate_t[e][:], ALU.is_gt, ALU.mult)
+        nc.vector.scalar_tensor_tensor(
+            m_tail[:], a_tail[:], 0.0, gate_tail[:, TAIL - HEAD_PART :].unsqueeze(1).to_broadcast([P, PACK, HEAD_PART]), ALU.is_gt, ALU.mult
+        )
+        turned_gate = psum.tile([P, PACK, P], F32, name="turned", tag="turned")
+        nc.tensor.transpose(turned_gate[:, 0, :], gate_rows[:], ident[:])
+        nc.scalar.copy(gate_cols[:], turned_gate[:, 0, 0 : S // P])
 
-        def gather_piece(e, lo, hi):
-            y = ring.tile([P, PACK, hi - lo], F32, name="y", bufs=3)
-            s0 = e * C + lo
+        def make_mask(e, block):
+            slots = slice(block * P, (block + 1) * P)
+            nc.scalar.activation(sign_t[e][:, :, slots], a_t[e][block // 2][:, :, (block % 2) * P : (block % 2 + 1) * P], ACT.Sign)
+            nc.gpsimd.tensor_scalar(
+                mask_t[e][:, slots, :], sign_t[e][:, :, slots].rearrange("p j s -> p s j"), 1.0, 0.0, ALU.min, ALU.max
+            )
+
+        def gather_plain(e):
+            picked = share.tile([P, PACK, widths[e]], F32, name="picked", tag="picked%d" % e, align_bytes=64)
+            for j in range(PACK):
+                nc.vector.tensor_copy(
+                    picked[:, j, :], dc[j][:].indirect(offs_t[:, e * C // 16 : (e * C + widths[e]) // 16])
+                )
+            return picked
+
+        def gate_and_round(e, picked):
+            blocks = C // P
+            banks = [psum.tile([P, 2, 2 * P], F32, name="back", tag="back") for n in range(blocks // 2)]
+            turned = {}
+
+            def turn(b, planes):
+                if b not in turned:
+                    turned[b] = psum.tile([P, PACK, P], F32, name="turned", tag="turned")
+                for j in planes:
+                    nc.tensor.transpose(turned[b][:, j, :], picked[:, j, b * P : (b + 1) * P], ident[:])
+
+            def gate_and_turn_back(b):
+                gated = ring.tile([P, 2, P, 2], BF16, name="gated", bufs=4)
+                block = e * blocks + b
+                nc.scalar.activation(
+                    gated[:],
+                    turned[b][:].rearrange("s (u d) p -> s u p d", u=2),
+                    ACT.Copy,
+                    scale=gate_cols[:, block : block + 1],
+                )
+                if e + 1 < E - 1:
+                    make_mask(e + 1, b)
+                words = gated[:].rearrange("s u p d -> s (u p d)").bitcast(F32)
+                place = slice((b % 2) * P, (b % 2 + 1) * P)
+                for u in range(2):
+                    nc.tensor.transpose(banks[b // 2][:, u, place], words[:, u * P : (u + 1) * P], ident[:])
+
+            for j in range(PACK):
+                for b in range(blocks):
+                    turn(b, [j])
+            for b in range(blocks):
+                gate_and_turn_back(b)
+            return banks
+
+        def mask_piece(e, banks):
+            da = ring.tile([P, widths[e], PACK], BF16, name="da", align_bytes=64, bufs=4)
+            for n, back in enumerate(banks):
+                slots = slice(2 * P * n, 2 * P * (n + 1))
+                nc.vector.tensor_tensor(
+                    da[:, slots, :].rearrange("p s (u d) -> p s u d", u=2),
+                    back[:].bitcast(BF16).rearrange("p u (s d) -> p s u d", d=2),
+                    mask_t[e][:, slots, :].rearrange("p s (u d) -> p s u d", u=2),
+                    ALU.mult,
+                )
+            return da
+
+        def make_masked_gate():
+            width = TAIL - HEAD_PART
+            nc.scalar.activation(sign_pool[:], a_pool[:], ACT.Sign)
+            for j in range(PACK):
+                nc.gpsimd.tensor_scalar(mask_pool[:, j, :], sign_pool[:, j, :], 1.0, 0.0, ALU.min, ALU.max)
+                nc.gpsimd.tensor_tensor(m_pool[:, j, :], mask_pool[:, j, :], gate_tail[:, :width], ALU.mult)
+
+        def gather_tail(y, lo, hi, factor):
+            s0 = S - TAIL + lo
             for j in range(PACK):
                 nc.vector.tensor_tensor(
-                    y[:, j, :], dc[j][:].indirect(offs_t[:, s0 // 16 : (s0 + hi - lo) // 16]), m_t[e][j][:, lo:hi], ALU.mult
+                    y[:, j, :], dc[j][:].indirect(offs_t[:, s0 // 16 : (s0 + hi - lo) // 16]), factor[:, j, :], ALU.mult
                 )
             return y
 
-        def round_piece(y, on_vector):
+        def round_piece(y, on_vector, tag):
             width = y.shape[2]
-            da = ring.tile([P, width, PACK], BF16, name="da", align_bytes=64, bufs=3)
+            da = share.tile([P, width, PACK], BF16, name="da", tag=tag, align_bytes=64)
             if on_vector:
-                nc.vector.tensor_copy(da[:], y[:].rearrange("p j s -> p s j"))
+                nc.vector.tensor_copy(da[:], y.rearrange("p j s -> p s j"))
             else:
-                nc.scalar.copy(da[:], y[:].rearrange("p j s -> p s j"))
+                nc.scalar.copy(da[:], y.rearrange("p j s -> p s j"))
             return da
 
         def quantize_piece(da, e, lo, hi):
             nc.vector.quantize_mx(
-                out=da_codes[e][:, lo:hi].bitcast(E5X4),
-                scales=da_scale[e][:, lo:hi],
+                out=da_codes[e][:, lead[e] + lo : lead[e] + hi].bitcast(E5X4),
+                scales=da_scale[e][:, lead[e] + lo : lead[e] + hi],
                 in_=da[:].rearrange("p s j -> p (s j)"),
             )
 
-        def expert_product(e, kt):
-            acc = psum.tile([P, C], F32, name="acc")
+        def product_pass(e, kt, first):
+            acc = psum.tile([P, C], F32, name="acc", tag="turned")
             nc.tensor.matmul_mx(
                 out=acc[:],
                 lhsT=w1_codes[:, e, 2 * P * kt : 2 * P * (kt + 1)].bitcast(FP4X4),
                 lhsT_scale=w1_scale[:, e, P * kt : P * (kt + 1)],
-                rhs=da_codes[e][:].bitcast(E5X4),
-                rhs_scale=da_scale[e][:],
+                rhs=da_codes[e][:, first : first + C].bitcast(E5X4),
+                rhs_scale=da_scale[e][:, first : first + C],
                 start=True,
                 stop=True,
             )
-            nc.scalar.copy(dx[kt][:, e * C : (e + 1) * C], acc[:])
+            return acc
 
-        pieces = [(0, 0, 512), (1, 0, 512), (2, 0, 512), (3, 0, 256), (3, 256, 384), (3, 384, 512)]
-        pending = None
-        for e, lo, hi in pieces:
-            if lo == 0:
-                for j in range(PACK):
-                    masked_gate(e, j)
-            y = gather_piece(e, lo, hi)
-            if pending is not None:
-                quantize_piece(*pending)
-                if pending[3] == C:
-                    expert_product(pending[1], 0)
-            pending = (round_piece(y, (e, hi) == (E - 1, C)), e, lo, hi)
-        quantize_piece(*pending)
-        expert_product(E - 1, 0)
+        def expert_product(e, kt):
+            nc.scalar.copy(dx[kt][:, e * C : (e + 1) * C], product_pass(e, kt, lead[e])[:])
+
+        for block in range(C // P):
+            make_mask(0, block)
+        make_masked_gate()
+        banks = []
+        for e in range(E - 1):
+            picked = gather_plain(e)
+            if e == E - 2:
+                for done in range(e):
+                    quantize_piece(mask_piece(done, banks[done]), done, 0, C)
+            banks.append(gate_and_round(e, picked))
+        expert_product(0, 0)
+        expert_product(1, 0)
+        cut = TAIL - HEAD_PART
+        half = cut + HEAD_PART // 2
+        y_a = share.tile([P, PACK, cut], F32, name="y_a", tag="after_mask1")
+        da_a = round_piece(gather_tail(y_a[:], 0, cut, m_pool[:]), False, "picked2")
+        y_b = share.tile([P, PACK, half - cut], F32, name="y_b", tag="after_mask0")
+        da_b = round_piece(gather_tail(y_b[:], cut, half, m_tail[:, :, : half - cut]), False, "picked1")
+        quantize_piece(mask_piece(E - 2, banks[E - 2]), E - 2, 0, C)
+        expert_product(E - 2, 0)
+        quantize_piece(da_a, E - 1, 0, cut)
+        ahead = [product_pass(e, 1, 0) for e in range(2)]
+        y_c = share.tile([P, PACK, TAIL - half], F32, name="y_c", tag="after_mask2")
+        y_last = gather_tail(y_c[:], half, TAIL, m_tail[:, :, half - cut :])
+        quantize_piece(da_b, E - 1, cut, half)
+        nc.scalar.copy(dx[0][:, S - C : S - P], product_pass(E - 1, 0, 0)[:, P:])
+        late = round_piece(y_last, True, "picked0")
+        quantize_piece(late, E - 1, half, C)
+        nc.vector.tensor_copy(dx[0][:, S - P :], product_pass(E - 1, 0, P)[:, C - P :])
+        for e in range(2):
+            nc.scalar.copy(dx[1][:, e * C : (e + 1) * C], ahead[e][:])
 
         def fetch(kt, lo, hi):
             first = ring.tile([P, hi - lo], F32, name="first", bufs=3)
@@ -179,7 +296,7 @@ def tile_moe_sdb_relu_kernel(
         waiting = None
         for kt, lo, hi in spans:
             if lo == 0 and kt + 1 < K // P:
-                for e in range(E):
+                for e in range(2 if kt == 0 else 0, E):
                     expert_product(e, kt + 1)
             pair = fetch(kt, lo, hi)
             if waiting is not None:

@@ -52,14 +52,11 @@ def tile_moe_sdb_relu_kernel(
         m_tail = keep.tile([P, PACK, HEAD_PART], F32, name="m_tail")
         widths = [C, C, C]
         a_pool = keep.tile([P, PACK, TAIL - HEAD_PART], F32, name="a_pool")
-        sign_pool = keep.tile([P, PACK, TAIL - HEAD_PART], BF16, name="sign_pool")
-        mask_pool = keep.tile([P, PACK, TAIL - HEAD_PART], BF16, name="mask_pool")
-        m_pool = keep.tile([P, PACK, TAIL - HEAD_PART], F32, name="m_pool")
         a_t = [
             [share.tile([P, PACK, C // 2], F32, name="a", tag="picked%d" % (h + 1) if e == 0 else "a%d_%d" % (e, h), align_bytes=64) for h in range(2)]
             for e in range(E - 1)
         ]
-        sign_t = [keep.tile([P, PACK, widths[e]], BF16, name="sign%d" % e) for e in range(E - 1)]
+        sign_t = [keep.tile([P, widths[e], PACK], BF16, name="sign%d" % e) for e in range(E - 1)]
         mask_t = [share.tile([P, widths[e], PACK], BF16, name="mask%d" % e, tag="after_mask%d" % e) for e in range(E - 1)]
         dc = [keep.tile([P, T], F32, name="dc%d" % j) for j in range(PACK)]
         dx = [keep.tile([P, S], F32, name="dx%d" % kt) for kt in range(K // P)]
@@ -94,16 +91,16 @@ def tile_moe_sdb_relu_kernel(
         nc.sync.dma_start(a_tail[:], a_rows[:, :, S - HEAD_PART :])
         nc.sync.dma_start(gate_rows[:], gate[0 : P * P // S, :].rearrange("r (c s) -> (r c) s", s=P))
         load_expert(0)
-        nc.sync.dma_start(gate_tail[:, : TAIL - HEAD_PART], gate[:, S - TAIL : S - HEAD_PART])
-        nc.sync.dma_start(a_pool[:], a_rows[:, :, S - TAIL : S - HEAD_PART])
         load_expert(1)
+        load_expert(2)
         for q in range(4):
             nc.sync.dma_start(
                 w1_scale[32 * q : 32 * q + 4, :, :].bitcast(I32),
                 w1t_scales[:, 0, 4 * q : 4 * q + 4, :].rearrange("e r k -> r e k").bitcast(I32),
             )
         nc.sync.dma_start(w1_codes[:].bitcast(I32), w1t_words[:, 0].rearrange("e p b -> p e b").bitcast(I32))
-        load_expert(2)
+        nc.sync.dma_start(gate_tail[:, : TAIL - HEAD_PART], gate[:, S - TAIL : S - HEAD_PART])
+        nc.sync.dma_start(a_pool[:], a_rows[:, :, S - TAIL : S - HEAD_PART])
         nc.sync.dma_start(pos1_t[:], pos1)
         nc.sync.dma_start(pos2_t[:], pos2)
 
@@ -141,10 +138,9 @@ def tile_moe_sdb_relu_kernel(
 
         def make_mask(e, block):
             slots = slice(block * P, (block + 1) * P)
-            nc.scalar.activation(sign_t[e][:, :, slots], a_t[e][block // 2][:, :, (block % 2) * P : (block % 2 + 1) * P], ACT.Sign)
-            nc.gpsimd.tensor_scalar(
-                mask_t[e][:, slots, :], sign_t[e][:, :, slots].rearrange("p j s -> p s j"), 1.0, 0.0, ALU.min, ALU.max
-            )
+            saved = a_t[e][block // 2][:, :, (block % 2) * P : (block % 2 + 1) * P]
+            nc.scalar.activation(sign_t[e][:, slots, :], saved.rearrange("p j s -> p s j"), ACT.Sign)
+            nc.gpsimd.tensor_scalar(mask_t[e][:, slots, :], sign_t[e][:, slots, :], 1.0, 0.0, ALU.min, ALU.max)
 
         def gather_plain(e):
             picked = share.tile([P, PACK, widths[e]], F32, name="picked", tag="picked%d" % e, align_bytes=64)
@@ -174,8 +170,8 @@ def tile_moe_sdb_relu_kernel(
                     ACT.Copy,
                     scale=gate_cols[:, block : block + 1],
                 )
-                if e + 1 < E - 1:
-                    make_mask(e + 1, b)
+                if e == 0:
+                    make_mask(1, b)
                 words = gated[:].rearrange("s u p d -> s (u p d)").bitcast(F32)
                 place = slice((b % 2) * P, (b % 2 + 1) * P)
                 for u in range(2):
@@ -199,13 +195,6 @@ def tile_moe_sdb_relu_kernel(
                     ALU.mult,
                 )
             return da
-
-        def make_masked_gate():
-            width = TAIL - HEAD_PART
-            nc.scalar.activation(sign_pool[:], a_pool[:], ACT.Sign)
-            for j in range(PACK):
-                nc.gpsimd.tensor_scalar(mask_pool[:, j, :], sign_pool[:, j, :], 1.0, 0.0, ALU.min, ALU.max)
-                nc.gpsimd.tensor_tensor(m_pool[:, j, :], mask_pool[:, j, :], gate_tail[:, :width], ALU.mult)
 
         def gather_tail(y, lo, hi, factor):
             s0 = S - TAIL + lo
@@ -249,22 +238,25 @@ def tile_moe_sdb_relu_kernel(
 
         for block in range(C // P):
             make_mask(0, block)
-        make_masked_gate()
-        banks = []
-        for e in range(E - 1):
-            picked = gather_plain(e)
-            if e == E - 2:
-                for done in range(e):
-                    quantize_piece(mask_piece(done, banks[done]), done, 0, C)
-            banks.append(gate_and_round(e, picked))
-        expert_product(0, 0)
-        expert_product(1, 0)
         cut = TAIL - HEAD_PART
         half = cut + HEAD_PART // 2
-        y_a = share.tile([P, PACK, cut], F32, name="y_a", tag="after_mask1")
-        da_a = round_piece(gather_tail(y_a[:], 0, cut, m_pool[:]), False, "picked2")
-        y_b = share.tile([P, PACK, half - cut], F32, name="y_b", tag="after_mask0")
-        da_b = round_piece(gather_tail(y_b[:], cut, half, m_tail[:, :, : half - cut]), False, "picked1")
+        banks = [gate_and_round(0, gather_plain(0))]
+        for block in range(C // P):
+            make_mask(2, block)
+        banks.append(gate_and_round(1, gather_plain(1)))
+        picked = gather_plain(2)
+        quantize_piece(mask_piece(0, banks[0]), 0, 0, C)
+        m_pool = share.tile([P, PACK, cut], F32, name="m_pool", tag="after_mask0")
+        nc.vector.scalar_tensor_tensor(
+            m_pool[:], a_pool[:], 0.0, gate_tail[:, :cut].unsqueeze(1).to_broadcast([P, PACK, cut]), ALU.is_gt, ALU.mult
+        )
+        quantize_piece(mask_piece(1, banks[1]), 1, 0, C)
+        banks.append(gate_and_round(2, picked))
+        expert_product(0, 0)
+        expert_product(1, 0)
+        y_ab = share.tile([P, PACK, half], F32, name="y_ab", tag="after_mask1")
+        da_a = round_piece(gather_tail(y_ab[:, :, :cut], 0, cut, m_pool[:]), False, "picked2")
+        da_b = round_piece(gather_tail(y_ab[:, :, cut:], cut, half, m_tail[:, :, : half - cut]), False, "picked1")
         quantize_piece(mask_piece(E - 2, banks[E - 2]), E - 2, 0, C)
         expert_product(E - 2, 0)
         quantize_piece(da_a, E - 1, 0, cut)

@@ -7,6 +7,11 @@ K, T, E, C, H, N = 512, 1024, 4, 512, 512, 512
 S = E * C
 P = 128
 PACK = 4
+BANK = 512
+BLOCKS = C // P
+TURNED = E - 1
+DIRECT = E - 1
+LIST_ROWS = 16
 FLOPS = 2 * N * H * T + 2 * H * K * S
 
 F32 = mybir.dt.float32
@@ -19,8 +24,6 @@ FP4X4 = mybir.dt.float4_e2m1fn_x4
 E5X4 = mybir.dt.float8_e5m2_x4
 ALU = mybir.AluOpType
 ACT = mybir.ActivationFunctionType
-TAIL = 512
-HEAD_PART = 256
 
 
 def tile_moe_sdb_relu_kernel(
@@ -29,13 +32,13 @@ def tile_moe_sdb_relu_kernel(
     nc = tc.nc
     with ExitStack() as ctx:
         keep = ctx.enter_context(tc.tile_pool(name="keep", bufs=1))
-        ring = ctx.enter_context(tc.tile_pool(name="ring", bufs=2))
-        share = ctx.enter_context(tc.tile_pool(name="share", bufs=1))
+        ring = ctx.enter_context(tc.tile_pool(name="ring", bufs=3))
+        reuse = ctx.enter_context(tc.tile_pool(name="reuse", bufs=1))
         psum = ctx.enter_context(tc.psum_pool(name="psum", bufs=4))
 
-        offs_t = keep.tile([P, S // 16], U16, name="offs_t")
-        pos1_t = keep.tile([P, T // 16], U16, name="pos1_t")
-        pos2_t = keep.tile([P, T // 16], U16, name="pos2_t")
+        offs_t = keep.tile([P, S // LIST_ROWS], U16, name="offs_t")
+        pos1_t = keep.tile([P, T // LIST_ROWS], U16, name="pos1_t")
+        pos2_t = keep.tile([P, T // LIST_ROWS], U16, name="pos2_t")
         w2_raw = keep.tile([P, 2 * H], U8, name="w2_raw", align_bytes=64)
         w2_codes = keep.tile([P, 2 * H], U8, name="w2_codes", align_bytes=64)
         w2s_raw = keep.tile([P, H], U8, name="w2s_raw", align_bytes=64)
@@ -47,60 +50,66 @@ def tile_moe_sdb_relu_kernel(
         ident = keep.tile([P, P], F32, name="ident")
         gate_rows = keep.tile([P, P], F32, name="gate_rows")
         gate_cols = keep.tile([P, S // P], F32, name="gate_cols")
-        gate_tail = keep.tile([P, TAIL], F32, name="gate_tail")
-        a_tail = keep.tile([P, PACK, HEAD_PART], F32, name="a_tail")
-        m_tail = keep.tile([P, PACK, HEAD_PART], F32, name="m_tail")
-        widths = [C, C, C]
-        a_pool = keep.tile([P, PACK, TAIL - HEAD_PART], F32, name="a_pool")
+        gate_direct = keep.tile([P, C], F32, name="gate_direct")
+        a_vector = keep.tile([P, PACK, 2 * P], F32, name="a_vector")
+        a_late = keep.tile([P, PACK, P], F32, name="a_late")
+        factor_early = keep.tile([P, PACK, 3 * P], F32, name="factor_early")
+        a_gpsimd = keep.tile([P, PACK, P], F32, name="a_gpsimd")
         a_t = [
-            [share.tile([P, PACK, C // 2], F32, name="a", tag="picked%d" % (h + 1) if e == 0 else "a%d_%d" % (e, h), align_bytes=64) for h in range(2)]
-            for e in range(E - 1)
+            [
+                reuse.tile(
+                    [P, PACK, C // 2],
+                    F32,
+                    name="a",
+                    tag="picked%d" % (h + 1) if e == 0 else "a%d_%d" % (e, h),
+                    align_bytes=64,
+                )
+                for h in range(2)
+            ]
+            for e in range(TURNED)
         ]
-        sign_t = [keep.tile([P, widths[e], PACK], BF16, name="sign%d" % e) for e in range(E - 1)]
-        mask_t = [share.tile([P, widths[e], PACK], BF16, name="mask%d" % e, tag="after_mask%d" % e) for e in range(E - 1)]
+        sign_t = [keep.tile([P, C, PACK], BF16, name="sign%d" % e) for e in range(TURNED)]
+        mask_t = [reuse.tile([P, C, PACK], BF16, name="mask%d" % e, tag="after_mask%d" % e) for e in range(TURNED)]
         dc = [keep.tile([P, T], F32, name="dc%d" % j) for j in range(PACK)]
         dx = [keep.tile([P, S], F32, name="dx%d" % kt) for kt in range(K // P)]
-        lead = [0] * (E - 1) + [P]
+        lead = [0] * TURNED + [P]
         da_codes = [keep.tile([P, lead[e] + C], U32, name="dac%d" % e, align_bytes=64) for e in range(E)]
         da_scale = [keep.tile([P, lead[e] + C], U8, name="das%d" % e, align_bytes=64) for e in range(E)]
 
         nc.gpsimd.memset(w2s_raw[:].bitcast(I32), 0)
         nc.gpsimd.memset(dy_scale[:].bitcast(I32), 0)
         nc.vector.memset(w1_scale[:].rearrange("p e k -> p (e k)").bitcast(I32), 0)
-        nc.vector.memset(da_codes[E - 1][:, :P].bitcast(I32), 0)
-        nc.vector.memset(da_scale[E - 1][:, :P].bitcast(I32), 0)
+        nc.vector.memset(da_codes[DIRECT][:, :P].bitcast(I32), 0)
+        nc.vector.memset(da_scale[DIRECT][:, :P].bitcast(I32), 0)
 
         a_rows = a.rearrange("(p j) s -> p j s", j=PACK)
+        direct0 = DIRECT * C
 
-        def load_scale_rows(queue, plane, rows, q):
-            queue.dma_start(plane[32 * q : 32 * q + 4, :].bitcast(I32), rows[4 * q : 4 * q + 4, :].bitcast(I32))
+        def load_scale_rows(plane, rows):
+            for q in range(4):
+                nc.sync.dma_start(plane[32 * q : 32 * q + 4, :].bitcast(I32), rows[4 * q : 4 * q + 4, :].bitcast(I32))
 
-        def load_expert(e):
-            for h in range(2):
-                nc.sync.dma_start(a_t[e][h][:], a_rows[:, :, e * C + h * C // 2 : e * C + (h + 1) * C // 2])
-
-        for q in range(4):
-            load_scale_rows(nc.sync, w2s_raw, w2t_scales[0], q)
         nc.sync.dma_start(w2_raw[:].bitcast(I32), w2t_words[0].bitcast(I32))
+        load_scale_rows(w2s_raw, w2t_scales[0])
         nc.sync.dma_start(dy_codes[:].bitcast(I32), dy_words[0].rearrange("p t d -> p (t d)").bitcast(I32))
-        for q in range(4):
-            load_scale_rows(nc.sync, dy_scale, dy_scales[0], q)
+        load_scale_rows(dy_scale, dy_scales[0])
         make_identity(nc, ident[:])
         nc.sync.dma_start(offs_t[:], offs)
-        nc.sync.dma_start(gate_tail[:, TAIL - HEAD_PART :], gate[:, S - HEAD_PART :])
-        nc.sync.dma_start(a_tail[:], a_rows[:, :, S - HEAD_PART :])
+        nc.sync.dma_start(gate_direct[:, : 3 * P], gate[:, direct0 : direct0 + 3 * P])
+        nc.sync.dma_start(a_vector[:], a_rows[:, :, direct0 + P : direct0 + 3 * P])
+        nc.sync.dma_start(a_gpsimd[:], a_rows[:, :, direct0 : direct0 + P])
         nc.sync.dma_start(gate_rows[:], gate[0 : P * P // S, :].rearrange("r (c s) -> (r c) s", s=P))
-        load_expert(0)
-        load_expert(1)
-        load_expert(2)
+        for e in range(TURNED):
+            for h in range(2):
+                nc.sync.dma_start(a_t[e][h][:], a_rows[:, :, e * C + h * C // 2 : e * C + (h + 1) * C // 2])
         for q in range(4):
             nc.sync.dma_start(
                 w1_scale[32 * q : 32 * q + 4, :, :].bitcast(I32),
                 w1t_scales[:, 0, 4 * q : 4 * q + 4, :].rearrange("e r k -> r e k").bitcast(I32),
             )
         nc.sync.dma_start(w1_codes[:].bitcast(I32), w1t_words[:, 0].rearrange("e p b -> p e b").bitcast(I32))
-        nc.sync.dma_start(gate_tail[:, : TAIL - HEAD_PART], gate[:, S - TAIL : S - HEAD_PART])
-        nc.sync.dma_start(a_pool[:], a_rows[:, :, S - TAIL : S - HEAD_PART])
+        nc.sync.dma_start(gate_direct[:, 3 * P :], gate[:, direct0 + 3 * P :])
+        nc.sync.dma_start(a_late[:], a_rows[:, :, direct0 + 3 * P :])
         nc.sync.dma_start(pos1_t[:], pos1)
         nc.sync.dma_start(pos2_t[:], pos2)
 
@@ -115,9 +124,9 @@ def tile_moe_sdb_relu_kernel(
             )
 
         for j in range(PACK):
-            for h in range(T // 512):
-                cols = slice(512 * h, 512 * (h + 1))
-                acc = psum.tile([P, 512], F32, name="acc", tag=("turned", "back")[h])
+            for h in range(T // BANK):
+                cols = slice(BANK * h, BANK * (h + 1))
+                acc = psum.tile([P, BANK], F32, name="acc", tag=("turned", "back")[h])
                 nc.tensor.matmul_mx(
                     out=acc[:],
                     lhsT=w2_codes[:, 2 * P * j : 2 * P * (j + 1)].bitcast(FP4X4),
@@ -129,9 +138,11 @@ def tile_moe_sdb_relu_kernel(
                 )
                 nc.scalar.copy(dc[j][:, cols], acc[:])
 
-        nc.vector.scalar_tensor_tensor(
-            m_tail[:], a_tail[:], 0.0, gate_tail[:, TAIL - HEAD_PART :].unsqueeze(1).to_broadcast([P, PACK, HEAD_PART]), ALU.is_gt, ALU.mult
-        )
+        def masked_gate(factor, saved, lo, hi):
+            spread = gate_direct[:, lo:hi].unsqueeze(1).to_broadcast([P, PACK, hi - lo])
+            nc.vector.scalar_tensor_tensor(factor, saved, 0.0, spread, ALU.is_gt, ALU.mult)
+
+        masked_gate(factor_early[:, :, P:], a_vector[:], P, 3 * P)
         turned_gate = psum.tile([P, PACK, P], F32, name="turned", tag="turned")
         nc.tensor.transpose(turned_gate[:, 0, :], gate_rows[:], ident[:])
         nc.scalar.copy(gate_cols[:], turned_gate[:, 0, 0 : S // P])
@@ -143,32 +154,28 @@ def tile_moe_sdb_relu_kernel(
             nc.gpsimd.tensor_scalar(mask_t[e][:, slots, :], sign_t[e][:, slots, :], 1.0, 0.0, ALU.min, ALU.max)
 
         def gather_plain(e):
-            picked = share.tile([P, PACK, widths[e]], F32, name="picked", tag="picked%d" % e, align_bytes=64)
+            picked = reuse.tile([P, PACK, C], F32, name="picked", tag="picked%d" % e, align_bytes=64)
+            entries = offs_t[:, e * C // LIST_ROWS : (e + 1) * C // LIST_ROWS]
             for j in range(PACK):
-                nc.vector.tensor_copy(
-                    picked[:, j, :], dc[j][:].indirect(offs_t[:, e * C // 16 : (e * C + widths[e]) // 16])
-                )
+                nc.vector.tensor_copy(picked[:, j, :], dc[j][:].indirect(entries))
             return picked
 
         def gate_and_round(e, picked):
-            blocks = C // P
-            banks = [psum.tile([P, 2, 2 * P], F32, name="back", tag="back") for n in range(blocks // 2)]
-            turned = {}
-
-            def turn(b, planes):
-                if b not in turned:
-                    turned[b] = psum.tile([P, PACK, P], F32, name="turned", tag="turned")
-                for j in planes:
+            banks = [psum.tile([P, 2, 2 * P], F32, name="back", tag="back") for n in range(BLOCKS // 2)]
+            turned = []
+            for j in range(PACK):
+                for b in range(BLOCKS):
+                    if j == 0:
+                        turned.append(psum.tile([P, PACK, P], F32, name="turned", tag="turned"))
                     nc.tensor.transpose(turned[b][:, j, :], picked[:, j, b * P : (b + 1) * P], ident[:])
-
-            def gate_and_turn_back(b):
-                gated = ring.tile([P, 2, P, 2], BF16, name="gated", bufs=4)
-                block = e * blocks + b
+            for b in range(BLOCKS):
+                gated = ring.tile([P, 2, P, 2], BF16, name="gated", bufs=BLOCKS)
+                column = e * BLOCKS + b
                 nc.scalar.activation(
                     gated[:],
                     turned[b][:].rearrange("s (u d) p -> s u p d", u=2),
                     ACT.Copy,
-                    scale=gate_cols[:, block : block + 1],
+                    scale=gate_cols[:, column : column + 1],
                 )
                 if e == 0:
                     make_mask(1, b)
@@ -176,16 +183,10 @@ def tile_moe_sdb_relu_kernel(
                 place = slice((b % 2) * P, (b % 2 + 1) * P)
                 for u in range(2):
                     nc.tensor.transpose(banks[b // 2][:, u, place], words[:, u * P : (u + 1) * P], ident[:])
-
-            for j in range(PACK):
-                for b in range(blocks):
-                    turn(b, [j])
-            for b in range(blocks):
-                gate_and_turn_back(b)
             return banks
 
-        def mask_piece(e, banks):
-            da = ring.tile([P, widths[e], PACK], BF16, name="da", align_bytes=64, bufs=4)
+        def apply_mask(e, banks):
+            da = ring.tile([P, C, PACK], BF16, name="da", align_bytes=64, bufs=4)
             for n, back in enumerate(banks):
                 slots = slice(2 * P * n, 2 * P * (n + 1))
                 nc.vector.tensor_tensor(
@@ -196,24 +197,17 @@ def tile_moe_sdb_relu_kernel(
                 )
             return da
 
-        def gather_tail(y, lo, hi, factor):
-            s0 = S - TAIL + lo
+        def gather_direct(product, lo, hi, factor):
+            entries = offs_t[:, (direct0 + lo) // LIST_ROWS : (direct0 + hi) // LIST_ROWS]
             for j in range(PACK):
-                nc.vector.tensor_tensor(
-                    y[:, j, :], dc[j][:].indirect(offs_t[:, s0 // 16 : (s0 + hi - lo) // 16]), factor[:, j, :], ALU.mult
-                )
-            return y
+                nc.vector.tensor_tensor(product[:, j, :], dc[j][:].indirect(entries), factor[:, j, :], ALU.mult)
 
-        def round_piece(y, on_vector, tag):
-            width = y.shape[2]
-            da = share.tile([P, width, PACK], BF16, name="da", tag=tag, align_bytes=64)
-            if on_vector:
-                nc.vector.tensor_copy(da[:], y.rearrange("p j s -> p s j"))
-            else:
-                nc.scalar.copy(da[:], y.rearrange("p j s -> p s j"))
+        def round_direct(product, copy, tag):
+            da = reuse.tile([P, product.shape[2], PACK], BF16, name="da", tag=tag, align_bytes=64)
+            copy(da[:], product.rearrange("p j s -> p s j"))
             return da
 
-        def quantize_piece(da, e, lo, hi):
+        def quantize(da, e, lo, hi):
             nc.vector.quantize_mx(
                 out=da_codes[e][:, lead[e] + lo : lead[e] + hi].bitcast(E5X4),
                 scales=da_scale[e][:, lead[e] + lo : lead[e] + hi],
@@ -236,62 +230,71 @@ def tile_moe_sdb_relu_kernel(
         def expert_product(e, kt):
             nc.scalar.copy(dx[kt][:, e * C : (e + 1) * C], product_pass(e, kt, lead[e])[:])
 
-        for block in range(C // P):
+        positive = keep.tile([P, PACK, P], F32, name="positive")
+        for j in range(0, PACK, 2):
+            nc.gpsimd.tensor_scalar(positive[:, j : j + 2, :], a_gpsimd[:, j : j + 2, :], 0.0, None, ALU.is_gt)
+            nc.gpsimd.tensor_tensor(
+                factor_early[:, j : j + 2, :P],
+                positive[:, j : j + 2, :],
+                gate_direct[:, :P].unsqueeze(1).to_broadcast([P, 2, P]),
+                ALU.mult,
+            )
+
+        for block in range(BLOCKS):
             make_mask(0, block)
-        cut = TAIL - HEAD_PART
-        half = cut + HEAD_PART // 2
         banks = [gate_and_round(0, gather_plain(0))]
-        for block in range(C // P):
+        for block in range(BLOCKS):
             make_mask(2, block)
         banks.append(gate_and_round(1, gather_plain(1)))
         picked = gather_plain(2)
-        quantize_piece(mask_piece(0, banks[0]), 0, 0, C)
-        m_pool = share.tile([P, PACK, cut], F32, name="m_pool", tag="after_mask0")
-        nc.vector.scalar_tensor_tensor(
-            m_pool[:], a_pool[:], 0.0, gate_tail[:, :cut].unsqueeze(1).to_broadcast([P, PACK, cut]), ALU.is_gt, ALU.mult
-        )
-        quantize_piece(mask_piece(1, banks[1]), 1, 0, C)
+        quantize(apply_mask(0, banks[0]), 0, 0, C)
+        product_01 = reuse.tile([P, PACK, 2 * P], F32, name="product_01", tag="after_mask0")
+        gather_direct(product_01[:], 0, 2 * P, factor_early[:, :, : 2 * P])
+        quantize(apply_mask(1, banks[1]), 1, 0, C)
         banks.append(gate_and_round(2, picked))
+        da_01 = round_direct(product_01[:], nc.scalar.copy, "picked2")
         expert_product(0, 0)
         expert_product(1, 0)
-        y_ab = share.tile([P, PACK, half], F32, name="y_ab", tag="after_mask1")
-        da_a = round_piece(gather_tail(y_ab[:, :, :cut], 0, cut, m_pool[:]), False, "picked2")
-        da_b = round_piece(gather_tail(y_ab[:, :, cut:], cut, half, m_tail[:, :, : half - cut]), False, "picked1")
-        quantize_piece(mask_piece(E - 2, banks[E - 2]), E - 2, 0, C)
-        expert_product(E - 2, 0)
-        quantize_piece(da_a, E - 1, 0, cut)
+        shared = reuse.tile([P, 2, PACK, P], F32, name="shared", tag="after_mask1")
+        product_2, factor_late = shared[:, 0], shared[:, 1]
+        masked_gate(factor_late, a_late[:], 3 * P, C)
+        gather_direct(product_2, 2 * P, 3 * P, factor_early[:, :, 2 * P :])
+        da_2 = round_direct(product_2, nc.scalar.copy, "picked1")
+        quantize(apply_mask(2, banks[2]), 2, 0, C)
+        expert_product(2, 0)
+        quantize(da_01, DIRECT, 0, 2 * P)
         ahead = [product_pass(e, 1, 0) for e in range(2)]
-        y_c = share.tile([P, PACK, TAIL - half], F32, name="y_c", tag="after_mask2")
-        y_last = gather_tail(y_c[:], half, TAIL, m_tail[:, :, half - cut :])
-        quantize_piece(da_b, E - 1, cut, half)
-        nc.scalar.copy(dx[0][:, S - C : S - P], product_pass(E - 1, 0, 0)[:, P:])
-        late = round_piece(y_last, True, "picked0")
-        quantize_piece(late, E - 1, half, C)
-        nc.vector.tensor_copy(dx[0][:, S - P :], product_pass(E - 1, 0, P)[:, C - P :])
-        for e in range(2):
-            nc.scalar.copy(dx[1][:, e * C : (e + 1) * C], ahead[e][:])
+        product_3 = reuse.tile([P, PACK, P], F32, name="product_3", tag="after_mask2")
+        gather_direct(product_3[:], 3 * P, C, factor_late)
+        quantize(da_2, DIRECT, 2 * P, 3 * P)
+        nc.scalar.copy(dx[0][:, direct0 : S - P], product_pass(DIRECT, 0, 0)[:, P:])
+        da_3 = round_direct(product_3[:], nc.vector.tensor_copy, "picked0")
+        quantize(da_3, DIRECT, 3 * P, C)
+        nc.vector.tensor_copy(dx[0][:, S - P :], product_pass(DIRECT, 0, P)[:, C - P :])
+        for e, acc in enumerate(ahead):
+            nc.scalar.copy(dx[1][:, e * C : (e + 1) * C], acc[:])
 
         def fetch(kt, lo, hi):
-            first = ring.tile([P, hi - lo], F32, name="first", bufs=3)
-            second = ring.tile([P, hi - lo], F32, name="second", bufs=3)
-            nc.vector.tensor_copy(first[:], dx[kt][:].indirect(pos1_t[:, lo // 16 : hi // 16]))
-            nc.vector.tensor_copy(second[:], dx[kt][:].indirect(pos2_t[:, lo // 16 : hi // 16]))
-            return first, second
+            first = ring.tile([P, hi - lo], F32, name="first")
+            second = ring.tile([P, hi - lo], F32, name="second")
+            nc.vector.tensor_copy(first[:], dx[kt][:].indirect(pos1_t[:, lo // LIST_ROWS : hi // LIST_ROWS]))
+            nc.vector.tensor_copy(second[:], dx[kt][:].indirect(pos2_t[:, lo // LIST_ROWS : hi // LIST_ROWS]))
+            return first, second, kt, lo, hi
 
-        def combine(first, second, kt, lo, hi, last):
-            total = ring.tile([P, hi - lo], F32, name="total", bufs=3)
-            engine = nc.vector if last else nc.gpsimd
+        def combine(engine, first, second, kt, lo, hi):
+            total = ring.tile([P, hi - lo], F32, name="total")
             engine.tensor_tensor(total[:], first[:], second[:], ALU.add)
             nc.sync.dma_start(out[kt * P : (kt + 1) * P, lo:hi], total[:])
 
-        spans = [(0, 0, 1024), (1, 0, 1024), (2, 0, 1024), (3, 0, 512), (3, 512, 768), (3, 768, 1024)]
-        waiting = None
+        last_tile = K // P - 1
+        spans = [(kt, 0, T) for kt in range(last_tile)]
+        spans += [(last_tile, 0, T // 2), (last_tile, T // 2, 3 * T // 4), (last_tile, 3 * T // 4, T)]
+        fetched = None
         for kt, lo, hi in spans:
-            if lo == 0 and kt + 1 < K // P:
-                for e in range(2 if kt == 0 else 0, E):
+            if kt < last_tile:
+                for e in range(len(ahead) if kt == 0 else 0, E):
                     expert_product(e, kt + 1)
-            pair = fetch(kt, lo, hi)
-            if waiting is not None:
-                combine(*waiting, False)
-            waiting = (pair[0], pair[1], kt, lo, hi)
-        combine(*waiting, True)
+            previous, fetched = fetched, fetch(kt, lo, hi)
+            if previous is not None:
+                combine(nc.gpsimd, *previous)
+        combine(nc.vector, *fetched)

from contextlib import ExitStack

import concourse.mybir as mybir
from concourse.masks import make_identity

K, T, E, C, H, N = 512, 1024, 4, 512, 512, 512
S = E * C
P = 128
PACK = 4
BANK = 512
BLOCKS = C // P
TURNED = E - 1
DIRECT = E - 1
LIST_ROWS = 16
FLOPS = 2 * N * H * T + 2 * H * K * S

F32 = mybir.dt.float32
BF16 = mybir.dt.bfloat16
I32 = mybir.dt.int32
U32 = mybir.dt.uint32
U16 = mybir.dt.uint16
U8 = mybir.dt.uint8
FP4X4 = mybir.dt.float4_e2m1fn_x4
E5X4 = mybir.dt.float8_e5m2_x4
ALU = mybir.AluOpType
ACT = mybir.ActivationFunctionType


def tile_moe_sdb_relu_kernel(
    tc, dy_words, dy_scales, w2t_words, w2t_scales, w1t_words, w1t_scales, a, gate, offs, pos1, pos2, out
):
    nc = tc.nc
    with ExitStack() as ctx:
        keep = ctx.enter_context(tc.tile_pool(name="keep", bufs=1))
        ring = ctx.enter_context(tc.tile_pool(name="ring", bufs=3))
        reuse = ctx.enter_context(tc.tile_pool(name="reuse", bufs=1))
        psum = ctx.enter_context(tc.psum_pool(name="psum", bufs=4))

        offs_t = keep.tile([P, S // LIST_ROWS], U16, name="offs_t")
        pos1_t = keep.tile([P, T // LIST_ROWS], U16, name="pos1_t")
        pos2_t = keep.tile([P, T // LIST_ROWS], U16, name="pos2_t")
        w2_raw = keep.tile([P, 2 * H], U8, name="w2_raw", align_bytes=64)
        w2_codes = keep.tile([P, 2 * H], U8, name="w2_codes", align_bytes=64)
        w2s_raw = keep.tile([P, H], U8, name="w2s_raw", align_bytes=64)
        w2_scale = keep.tile([P, H], U8, name="w2_scale", align_bytes=64)
        dy_codes = keep.tile([P, T], U32, name="dy_codes", align_bytes=64)
        dy_scale = keep.tile([P, T], U8, name="dy_scale", align_bytes=64)
        w1_codes = keep.tile([P, E, 2 * K], U8, name="w1_codes", align_bytes=64)
        w1_scale = keep.tile([P, E, K], U8, name="w1_scale", align_bytes=64)
        ident = keep.tile([P, P], F32, name="ident")
        gate_rows = keep.tile([P, P], F32, name="gate_rows")
        gate_cols = keep.tile([P, S // P], F32, name="gate_cols")
        gate_direct = keep.tile([P, C], F32, name="gate_direct")
        a_vector = keep.tile([P, PACK, 2 * P], F32, name="a_vector")
        a_late = keep.tile([P, PACK, P], F32, name="a_late")
        factor_early = keep.tile([P, PACK, 3 * P], F32, name="factor_early")
        a_gpsimd = keep.tile([P, PACK, P], F32, name="a_gpsimd")
        a_t = [
            [
                reuse.tile(
                    [P, PACK, C // 2],
                    F32,
                    name="a",
                    tag="picked%d" % (h + 1) if e == 0 else "a%d_%d" % (e, h),
                    align_bytes=64,
                )
                for h in range(2)
            ]
            for e in range(TURNED)
        ]
        sign_t = [keep.tile([P, C, PACK], BF16, name="sign%d" % e) for e in range(TURNED)]
        mask_t = [reuse.tile([P, C, PACK], BF16, name="mask%d" % e, tag="after_mask%d" % e) for e in range(TURNED)]
        dc = [keep.tile([P, T], F32, name="dc%d" % j) for j in range(PACK)]
        dx = [keep.tile([P, S], F32, name="dx%d" % kt) for kt in range(K // P)]
        lead = [0] * TURNED + [P]
        da_codes = [keep.tile([P, lead[e] + C], U32, name="dac%d" % e, align_bytes=64) for e in range(E)]
        da_scale = [keep.tile([P, lead[e] + C], U8, name="das%d" % e, align_bytes=64) for e in range(E)]

        nc.gpsimd.memset(w2s_raw[:].bitcast(I32), 0)
        nc.gpsimd.memset(dy_scale[:].bitcast(I32), 0)
        nc.vector.memset(w1_scale[:].rearrange("p e k -> p (e k)").bitcast(I32), 0)
        nc.vector.memset(da_codes[DIRECT][:, :P].bitcast(I32), 0)
        nc.vector.memset(da_scale[DIRECT][:, :P].bitcast(I32), 0)

        a_rows = a.rearrange("(p j) s -> p j s", j=PACK)
        direct0 = DIRECT * C

        def load_scale_rows(plane, rows):
            for q in range(4):
                nc.sync.dma_start(plane[32 * q : 32 * q + 4, :].bitcast(I32), rows[4 * q : 4 * q + 4, :].bitcast(I32))

        nc.sync.dma_start(w2_raw[:].bitcast(I32), w2t_words[0].bitcast(I32))
        load_scale_rows(w2s_raw, w2t_scales[0])
        nc.sync.dma_start(dy_codes[:].bitcast(I32), dy_words[0].rearrange("p t d -> p (t d)").bitcast(I32))
        load_scale_rows(dy_scale, dy_scales[0])
        make_identity(nc, ident[:])
        nc.sync.dma_start(offs_t[:], offs)
        nc.sync.dma_start(gate_direct[:, : 3 * P], gate[:, direct0 : direct0 + 3 * P])
        nc.sync.dma_start(a_vector[:], a_rows[:, :, direct0 + P : direct0 + 3 * P])
        nc.sync.dma_start(a_gpsimd[:], a_rows[:, :, direct0 : direct0 + P])
        nc.sync.dma_start(gate_rows[:], gate[0 : P * P // S, :].rearrange("r (c s) -> (r c) s", s=P))
        for e in range(TURNED):
            for h in range(2):
                nc.sync.dma_start(a_t[e][h][:], a_rows[:, :, e * C + h * C // 2 : e * C + (h + 1) * C // 2])
        for q in range(4):
            nc.sync.dma_start(
                w1_scale[32 * q : 32 * q + 4, :, :].bitcast(I32),
                w1t_scales[:, 0, 4 * q : 4 * q + 4, :].rearrange("e r k -> r e k").bitcast(I32),
            )
        nc.sync.dma_start(w1_codes[:].bitcast(I32), w1t_words[:, 0].rearrange("e p b -> p e b").bitcast(I32))
        nc.sync.dma_start(gate_direct[:, 3 * P :], gate[:, direct0 + 3 * P :])
        nc.sync.dma_start(a_late[:], a_rows[:, :, direct0 + 3 * P :])
        nc.sync.dma_start(pos1_t[:], pos1)
        nc.sync.dma_start(pos2_t[:], pos2)

        for lo, hi in ((0, 1), (1, PACK)):
            nc.vector.tensor_copy(
                w2_codes[:].bitcast(U16).rearrange("p (j m) -> p j m", j=PACK)[:, lo:hi, :],
                w2_raw[:].bitcast(U16).rearrange("p (m j) -> p j m", j=PACK)[:, lo:hi, :],
            )
            nc.vector.tensor_copy(
                w2_scale[:].rearrange("p (j m) -> p j m", j=PACK)[:, lo:hi, :],
                w2s_raw[:].rearrange("p (m j) -> p j m", j=PACK)[:, lo:hi, :],
            )

        for j in range(PACK):
            for h in range(T // BANK):
                cols = slice(BANK * h, BANK * (h + 1))
                acc = psum.tile([P, BANK], F32, name="acc", tag=("turned", "back")[h])
                nc.tensor.matmul_mx(
                    out=acc[:],
                    lhsT=w2_codes[:, 2 * P * j : 2 * P * (j + 1)].bitcast(FP4X4),
                    lhsT_scale=w2_scale[:, P * j : P * (j + 1)],
                    rhs=dy_codes[:, cols].bitcast(E5X4),
                    rhs_scale=dy_scale[:, cols],
                    start=True,
                    stop=True,
                )
                nc.scalar.copy(dc[j][:, cols], acc[:])

        def masked_gate(factor, saved, lo, hi):
            spread = gate_direct[:, lo:hi].unsqueeze(1).to_broadcast([P, PACK, hi - lo])
            nc.vector.scalar_tensor_tensor(factor, saved, 0.0, spread, ALU.is_gt, ALU.mult)

        masked_gate(factor_early[:, :, P:], a_vector[:], P, 3 * P)
        turned_gate = psum.tile([P, PACK, P], F32, name="turned", tag="turned")
        nc.tensor.transpose(turned_gate[:, 0, :], gate_rows[:], ident[:])
        nc.scalar.copy(gate_cols[:], turned_gate[:, 0, 0 : S // P])

        def make_mask(e, block):
            slots = slice(block * P, (block + 1) * P)
            saved = a_t[e][block // 2][:, :, (block % 2) * P : (block % 2 + 1) * P]
            nc.scalar.activation(sign_t[e][:, slots, :], saved.rearrange("p j s -> p s j"), ACT.Sign)
            nc.gpsimd.tensor_scalar(mask_t[e][:, slots, :], sign_t[e][:, slots, :], 1.0, 0.0, ALU.min, ALU.max)

        def gather_plain(e):
            picked = reuse.tile([P, PACK, C], F32, name="picked", tag="picked%d" % e, align_bytes=64)
            entries = offs_t[:, e * C // LIST_ROWS : (e + 1) * C // LIST_ROWS]
            for j in range(PACK):
                nc.vector.tensor_copy(picked[:, j, :], dc[j][:].indirect(entries))
            return picked

        def gate_and_round(e, picked):
            banks = [psum.tile([P, 2, 2 * P], F32, name="back", tag="back") for n in range(BLOCKS // 2)]
            turned = []
            for j in range(PACK):
                for b in range(BLOCKS):
                    if j == 0:
                        turned.append(psum.tile([P, PACK, P], F32, name="turned", tag="turned"))
                    nc.tensor.transpose(turned[b][:, j, :], picked[:, j, b * P : (b + 1) * P], ident[:])
            for b in range(BLOCKS):
                gated = ring.tile([P, 2, P, 2], BF16, name="gated", bufs=BLOCKS)
                column = e * BLOCKS + b
                nc.scalar.activation(
                    gated[:],
                    turned[b][:].rearrange("s (u d) p -> s u p d", u=2),
                    ACT.Copy,
                    scale=gate_cols[:, column : column + 1],
                )
                if e == 0:
                    make_mask(1, b)
                words = gated[:].rearrange("s u p d -> s (u p d)").bitcast(F32)
                place = slice((b % 2) * P, (b % 2 + 1) * P)
                for u in range(2):
                    nc.tensor.transpose(banks[b // 2][:, u, place], words[:, u * P : (u + 1) * P], ident[:])
            return banks

        def apply_mask(e, banks):
            da = ring.tile([P, C, PACK], BF16, name="da", align_bytes=64, bufs=4)
            for n, back in enumerate(banks):
                slots = slice(2 * P * n, 2 * P * (n + 1))
                nc.vector.tensor_tensor(
                    da[:, slots, :].rearrange("p s (u d) -> p s u d", u=2),
                    back[:].bitcast(BF16).rearrange("p u (s d) -> p s u d", d=2),
                    mask_t[e][:, slots, :].rearrange("p s (u d) -> p s u d", u=2),
                    ALU.mult,
                )
            return da

        def gather_direct(product, lo, hi, factor):
            entries = offs_t[:, (direct0 + lo) // LIST_ROWS : (direct0 + hi) // LIST_ROWS]
            for j in range(PACK):
                nc.vector.tensor_tensor(product[:, j, :], dc[j][:].indirect(entries), factor[:, j, :], ALU.mult)

        def round_direct(product, copy, tag):
            da = reuse.tile([P, product.shape[2], PACK], BF16, name="da", tag=tag, align_bytes=64)
            copy(da[:], product.rearrange("p j s -> p s j"))
            return da

        def quantize(da, e, lo, hi):
            nc.vector.quantize_mx(
                out=da_codes[e][:, lead[e] + lo : lead[e] + hi].bitcast(E5X4),
                scales=da_scale[e][:, lead[e] + lo : lead[e] + hi],
                in_=da[:].rearrange("p s j -> p (s j)"),
            )

        def product_pass(e, kt, first):
            acc = psum.tile([P, C], F32, name="acc", tag="turned")
            nc.tensor.matmul_mx(
                out=acc[:],
                lhsT=w1_codes[:, e, 2 * P * kt : 2 * P * (kt + 1)].bitcast(FP4X4),
                lhsT_scale=w1_scale[:, e, P * kt : P * (kt + 1)],
                rhs=da_codes[e][:, first : first + C].bitcast(E5X4),
                rhs_scale=da_scale[e][:, first : first + C],
                start=True,
                stop=True,
            )
            return acc

        def expert_product(e, kt):
            nc.scalar.copy(dx[kt][:, e * C : (e + 1) * C], product_pass(e, kt, lead[e])[:])

        positive = keep.tile([P, PACK, P], F32, name="positive")
        for j in range(0, PACK, 2):
            nc.gpsimd.tensor_scalar(positive[:, j : j + 2, :], a_gpsimd[:, j : j + 2, :], 0.0, None, ALU.is_gt)
            nc.gpsimd.tensor_tensor(
                factor_early[:, j : j + 2, :P],
                positive[:, j : j + 2, :],
                gate_direct[:, :P].unsqueeze(1).to_broadcast([P, 2, P]),
                ALU.mult,
            )

        for block in range(BLOCKS):
            make_mask(0, block)
        banks = [gate_and_round(0, gather_plain(0))]
        for block in range(BLOCKS):
            make_mask(2, block)
        banks.append(gate_and_round(1, gather_plain(1)))
        picked = gather_plain(2)
        quantize(apply_mask(0, banks[0]), 0, 0, C)
        product_01 = reuse.tile([P, PACK, 2 * P], F32, name="product_01", tag="after_mask0")
        gather_direct(product_01[:], 0, 2 * P, factor_early[:, :, : 2 * P])
        quantize(apply_mask(1, banks[1]), 1, 0, C)
        banks.append(gate_and_round(2, picked))
        da_01 = round_direct(product_01[:], nc.scalar.copy, "picked2")
        expert_product(0, 0)
        expert_product(1, 0)
        shared = reuse.tile([P, 2, PACK, P], F32, name="shared", tag="after_mask1")
        product_2, factor_late = shared[:, 0], shared[:, 1]
        masked_gate(factor_late, a_late[:], 3 * P, C)
        gather_direct(product_2, 2 * P, 3 * P, factor_early[:, :, 2 * P :])
        da_2 = round_direct(product_2, nc.scalar.copy, "picked1")
        quantize(apply_mask(2, banks[2]), 2, 0, C)
        expert_product(2, 0)
        quantize(da_01, DIRECT, 0, 2 * P)
        ahead = [product_pass(e, 1, 0) for e in range(2)]
        product_3 = reuse.tile([P, PACK, P], F32, name="product_3", tag="after_mask2")
        gather_direct(product_3[:], 3 * P, C, factor_late)
        quantize(da_2, DIRECT, 2 * P, 3 * P)
        nc.scalar.copy(dx[0][:, direct0 : S - P], product_pass(DIRECT, 0, 0)[:, P:])
        da_3 = round_direct(product_3[:], nc.vector.tensor_copy, "picked0")
        quantize(da_3, DIRECT, 3 * P, C)
        nc.vector.tensor_copy(dx[0][:, S - P :], product_pass(DIRECT, 0, P)[:, C - P :])
        for e, acc in enumerate(ahead):
            nc.scalar.copy(dx[1][:, e * C : (e + 1) * C], acc[:])

        def fetch(kt, lo, hi):
            first = ring.tile([P, hi - lo], F32, name="first")
            second = ring.tile([P, hi - lo], F32, name="second")
            nc.vector.tensor_copy(first[:], dx[kt][:].indirect(pos1_t[:, lo // LIST_ROWS : hi // LIST_ROWS]))
            nc.vector.tensor_copy(second[:], dx[kt][:].indirect(pos2_t[:, lo // LIST_ROWS : hi // LIST_ROWS]))
            return first, second, kt, lo, hi

        def combine(engine, first, second, kt, lo, hi):
            total = ring.tile([P, hi - lo], F32, name="total")
            engine.tensor_tensor(total[:], first[:], second[:], ALU.add)
            nc.sync.dma_start(out[kt * P : (kt + 1) * P, lo:hi], total[:])

        last_tile = K // P - 1
        spans = [(kt, 0, T) for kt in range(last_tile)]
        spans += [(last_tile, 0, T // 2), (last_tile, T // 2, 3 * T // 4), (last_tile, 3 * T // 4, T)]
        fetched = None
        for kt, lo, hi in spans:
            if kt < last_tile:
                for e in range(len(ahead) if kt == 0 else 0, E):
                    expert_product(e, kt + 1)
            previous, fetched = fetched, fetch(kt, lo, hi)
            if previous is not None:
                combine(nc.gpsimd, *previous)
        combine(nc.vector, *fetched)
